import numpy as np, ml_dtypes
CORES = [5,21,45,77,85,101,109,125,133,141,189,213]
N = 12
import mx_ref
NC = 256
SEQ = [0,0,0,0,1,2,3,3,4,4,5,5]
WID = [244,160,242,182,202,132,256,178,168,128,210,130]
BF = ml_dtypes.bfloat16
def setup_inputs(rng):
    def f(*shape):
        return mx_ref.flush((rng.standard_normal(shape, dtype=np.float32) * np.exp2(rng.integers(-2, 3, shape[:-1] + (1,)))).astype(BF))
    return {"w": f(N, 128, 512), "x": f(N, 128, 4 * NC)}
def setup_inputs_blocks(rng):
    d = setup_inputs(rng)
    for k in ("w", "x"): d[k] = mx_ref.spread(d[k], rng, 4)
    return d
def setup_inputs_wide(rng):
    d = setup_inputs(rng)
    for k in ("w", "x"): d[k] = mx_ref.flush((d[k].astype(np.float32) * np.exp2(rng.integers(-10, 11, (N, 1, 1))).astype(np.float32)).astype(BF))
    return d
def reference(w, x):
    y = np.full((N, 128, 828), np.nan, np.float32)
    for r in range(N):
        qw = mx_ref.quantize(w[r]); a = 0
        for j in range(N):
            if SEQ[j] == SEQ[r]:
                y[r][:, a:a + WID[j]] = mx_ref.matmul(qw, mx_ref.quantize(x[j][:, :4 * WID[j]])); a += WID[j]
    return {"y": y}

@@ -1,0 +1,182 @@
+from concourse.bass import DstId, RemoteDMATransfer
+from concourse.mybir import dt, ActivationFunctionType
+
+NSIM = 256
+SLOT = 256
+NSLOT = 4
+BANK = 512
+YW = 828
+
+SCRATCH = {
+    "xt": ("sbuf", [128, 4 * SLOT], "bfloat16"),
+    "wt": ("sbuf", [128, 512], "bfloat16"),
+    "wq": ("sbuf", [128, 128], "float8_e4m3fn_x4"),
+    "ws": ("sbuf", [128, 128], "uint8"),
+    "xq": ("sbuf", [128, NSLOT * SLOT], "float8_e4m3fn_x4"),
+    "xs": ("sbuf", [128, NSLOT * SLOT], "uint8"),
+    "yb": ("sbuf", [128, YW], "float32"),
+    "ps": ("psum", [128, NSLOT * BANK], "float32"),
+}
+SEMAPHORES = (["lx", "lw", "qx", "qw", "hin", "sent", "st0", "st1"]
+              + ["arr%d" % k for k in range(NSLOT)]
+              + ["mm%d" % k for k in range(NSLOT)]
+              + ["cp%d" % k for k in range(NSLOT)])
+
+
+def _engines(mask):
+    return [e for e in range(mask.bit_length()) if (mask >> e) & 1]
+
+
+def _mask(engs):
+    m = 0
+    for e in engs:
+        m |= 1 << e
+    return m
+
+
+def _plan(T, topo):
+    cores, seq = list(T.cores), T.tables["SEQ"]
+    n = len(cores)
+
+    def peers(j):
+        return [d for d in range(n) if d != j and seq[d] == seq[j]]
+
+    far = [[d for d in peers(j) if not topo.may_write(cores[j], cores[d])] for j in range(n)]
+    routes = {}
+    for j in range(n):
+        home = cores[j]
+        for d in peers(j):
+            if d not in far[j]:
+                routes[(j, d)] = None
+                continue
+            i = far[j].index(d)
+            p = [s for s in peers(d) if d in far[s]].index(j)
+            able = [c for c in range(NSIM) if c not in cores
+                    and topo.host(c) == topo.host(home) and topo.chip(c) == topo.chip(home)
+                    and topo.may_write(home, c) and topo.may_write(c, cores[d])]
+            own = [c for c in able if topo.die(c) == topo.die(home)]
+            other = [c for c in able if topo.die(c) != topo.die(home)]
+            pick = own if (i + p) % 2 == 0 else other
+            routes[(j, d)] = (pick[0], pick[1])
+    return routes
+
+
+def _share(topo, src, dst, t):
+    return _engines(topo.mask(src, dst))[t % 2::2]
+
+
+def rank_program(g, core, T, topo):
+    cores, seq, wid = list(T.cores), T.tables["SEQ"], T.tables["WID"]
+    n = len(cores)
+    S = T.sem
+    routes = _plan(T, topo)
+
+    def members(j):
+        return [r for r in range(n) if seq[r] == seq[j]]
+
+    def slot(j):
+        return members(j).index(j)
+
+    def piece(j, part):
+        a = slot(j) * SLOT
+        if part == 0:
+            return T.xq[:, a:a + wid[j]].bitcast(dt.uint8)
+        return T.xs[:, a:a + wid[j]]
+
+    rank = T.rank_of(core)
+
+    if rank is None:
+        for (j, d), h in routes.items():
+            if h is None or core not in h:
+                continue
+            part = h.index(core)
+            t = [x for x in members(j) if x != j and routes[(j, x)] is not None].index(d)
+            rid, pid = topo.addr(cores[d], core)
+            m = topo.mask(core, cores[d])
+            g.wait_ge(S.hin, len(_share(topo, cores[j], core, t)))
+            g.remote_dma(piece(j, part), piece(j, part), S["arr%d" % slot(j)], S.sent, pid, rid, m)
+            g.wait_ge(S.sent, len(_engines(m)))
+        return
+
+    j, W = rank, wid[rank]
+    a = slot(j) * SLOT
+    others = [d for d in members(j) if d != j]
+    relay = [d for d in others if routes[(j, d)] is not None]
+    direct = [d for d in others if routes[(j, d)] is None]
+
+    g.sync.dma_start(T.xt[:, :4 * W], T.x[:, :4 * W]).then_inc(S.lx, 16)
+    g.sync.dma_start(T.wt[:, :], T.w[:, :]).then_inc(S.lw, 16)
+
+    g.vector.wait_ge(S.lx, 16)
+    g.vector.quantize_mx(T.xq[:, a:a + W], T.xs[:, a:a + W], T.xt[:, :4 * W]).then_inc(S.qx, 1)
+    g.vector.wait_ge(S.lw, 16)
+    g.vector.quantize_mx(T.wq[:, :], T.ws[:, :], T.wt[:, :]).then_inc(S.qw, 1)
+
+    sent = 0
+    if others:
+        g.wait_ge(S.qx, 1)
+    if relay:
+        for part in (0, 1):
+            trs = []
+            for t, d in enumerate(relay):
+                h = routes[(j, d)][part]
+                rid, pid = topo.addr(h, core)
+                engs = _share(topo, core, h, t)
+                trs.append(RemoteDMATransfer(dst_ids=[DstId(rid=rid, pnc=pid)], dma_engine_mask=_mask(engs),
+                                             remote_sem=S.hin, src=piece(j, part), dst=piece(j, part)))
+                sent += len(engs)
+            g.remote_dma_fused(trs, local_sem=S.sent)
+    for part in (0, 1):
+        for d in direct:
+            rid, pid = topo.addr(cores[d], core)
+            m = topo.mask(core, cores[d])
+            g.remote_dma(piece(j, part), piece(j, part), S["arr%d" % slot(j)], S.sent, pid, rid, m)
+            sent += len(_engines(m))
+
+    need = {}
+    for s in others:
+        h = routes[(s, j)]
+        if h is None:
+            need[s] = 2 * len(_engines(topo.mask(cores[s], core)))
+        else:
+            need[s] = sum(len(_engines(topo.mask(c, core))) for c in h)
+
+    order = ([j] + sorted([s for s in others if routes[(s, j)] is None], key=lambda s: wid[s])
+             + sorted([s for s in others if routes[(s, j)] is not None], key=lambda s: wid[s]))
+
+    g.tensor.wait_ge(S.qw, 1)
+    g.tensor.wait_ge(S.qx, 1)
+    for s in order:
+        k = slot(s)
+        if s != j:
+            g.tensor.wait_ge(S["arr%d" % k], need[s])
+        g.tensor.matmul_mx(T.ps[:, BANK * k:BANK * k + wid[s]], T.wq[:, :], T.ws[:, :],
+                           T.xq[:, SLOT * k:SLOT * k + wid[s]], T.xs[:, SLOT * k:SLOT * k + wid[s]],
+                           True, True).then_inc(S["mm%d" % k], 1)
+
+    stores = [0, 0]
+    for idx, s in enumerate(order):
+        k = slot(s)
+        o = sum(wid[r] for r in members(j) if r < s)
+        bank = T.ps[:, BANK * k:BANK * k + wid[s]]
+        block = T.yb[:, o:o + wid[s]]
+        lane = idx % 2
+        if lane == 0:
+            g.vector.wait_ge(S["mm%d" % k], 1)
+            g.vector.tensor_copy(block, bank).then_inc(S["cp%d" % k], 1)
+            q, st = g.sync, S.st0
+        else:
+            g.scalar.wait_ge(S["mm%d" % k], 1)
+            g.scalar.activation(block, bank, ActivationFunctionType.Copy).then_inc(S["cp%d" % k], 1)
+            q, st = g.scalar, S.st1
+        q.wait_ge(S["cp%d" % k], 1)
+        if stores[lane] == 0 and sent:
+            q.wait_ge(S.sent, sent)
+        q.dma_start(T.y[:, o:o + wid[s]], T.yb[:, o:o + wid[s]]).then_inc(st, 16)
+        stores[lane] += 1
+
+    g.sync.wait_ge(S.st0, 16 * stores[0])
+    if stores[1]:
+        g.scalar.wait_ge(S.st1, 16 * stores[1])
+    if sent:
+        g.wait_ge(S.sent, sent)

@@ -6,6 +6,8 @@ SLOT = 256
 NSLOT = 4
 BANK = 512
 YW = 828
+LEAST = 128
+MINP2 = 32
 
 SCRATCH = {
     "xt": ("sbuf", [128, 4 * SLOT], "bfloat16"),
@@ -14,13 +16,15 @@ SCRATCH = {
     "ws": ("sbuf", [128, 128], "uint8"),
     "xq": ("sbuf", [128, NSLOT * SLOT], "float8_e4m3fn_x4"),
     "xs": ("sbuf", [128, NSLOT * SLOT], "uint8"),
+    "xq2": ("sbuf", [128, LEAST], "float8_e4m3fn_x4"),
+    "xs2": ("sbuf", [128, LEAST], "uint8"),
+    "xq3": ("sbuf", [128, SLOT], "float8_e4m3fn_x4"),
+    "xs3": ("sbuf", [128, SLOT], "uint8"),
     "yb": ("sbuf", [128, YW], "float32"),
-    "ps": ("psum", [128, NSLOT * BANK], "float32"),
+    "ps": ("psum", [128, 2 * NSLOT * BANK], "float32"),
 }
-SEMAPHORES = (["lx", "lw", "qx", "qw", "hin", "sent", "st0", "st1"]
-              + ["arr%d" % k for k in range(NSLOT)]
-              + ["mm%d" % k for k in range(NSLOT)]
-              + ["cp%d" % k for k in range(NSLOT)])
+SEMAPHORES = (["lx", "lx2", "lw", "q0", "q1", "q2", "qw", "hin0", "hin1", "sentr", "sentd", "st0", "st1"]
+              + ["%s%d_%d" % (nm, k, p) for nm in ("arr", "mm", "cp") for k in range(NSLOT) for p in range(2)])
 
 
 def _engines(mask):
@@ -77,11 +81,16 @@ def rank_program(g, core, T, topo):
     def slot(j):
         return members(j).index(j)
 
-    def piece(j, part):
+    def pieces(j):
+        if wid[j] - LEAST < MINP2 or not [d for d in members(j) if d != j and routes[(j, d)] is not None]:
+            return [(0, wid[j])]
+        return [(0, LEAST), (LEAST, wid[j])]
+
+    def land(j, run, part):
         a = slot(j) * SLOT
         if part == 0:
-            return T.xq[:, a:a + wid[j]].bitcast(dt.uint8)
-        return T.xs[:, a:a + wid[j]]
+            return T.xq[:, a + run[0]:a + run[1]].bitcast(dt.uint8)
+        return T.xs[:, a + run[0]:a + run[1]]
 
     rank = T.rank_of(core)
 
@@ -93,45 +102,72 @@ def rank_program(g, core, T, topo):
             t = [x for x in members(j) if x != j and routes[(j, x)] is not None].index(d)
             rid, pid = topo.addr(cores[d], core)
             m = topo.mask(core, cores[d])
-            g.wait_ge(S.hin, len(_share(topo, cores[j], core, t)))
-            g.remote_dma(piece(j, part), piece(j, part), S["arr%d" % slot(j)], S.sent, pid, rid, m)
-            g.wait_ge(S.sent, len(_engines(m)))
+            for p, run in enumerate(pieces(j)):
+                g.wait_ge(S["hin%d" % p], len(_share(topo, cores[j], core, t)))
+                g.remote_dma(land(j, run, part), land(j, run, part), S["arr%d_%d" % (slot(j), p)], S.sentr, pid, rid, m)
+            g.wait_ge(S.sentr, len(pieces(j)) * len(_engines(m)))
         return
 
     j, W = rank, wid[rank]
     a = slot(j) * SLOT
+    split = len(pieces(j)) == 2
     others = [d for d in members(j) if d != j]
     relay = [d for d in others if routes[(j, d)] is not None]
     direct = [d for d in others if routes[(j, d)] is None]
+    first = pieces(j)[0][1]
 
-    g.sync.dma_start(T.xt[:, :4 * W], T.x[:, :4 * W]).then_inc(S.lx, 16)
+    g.sync.dma_start(T.xt[:, :4 * first], T.x[:, :4 * first]).then_inc(S.lx, 16)
+    if split:
+        g.scalar.dma_start(T.xt[:, 4 * first:4 * W], T.x[:, 4 * first:4 * W]).then_inc(S.lx2, 16)
     g.sync.dma_start(T.wt[:, :], T.w[:, :]).then_inc(S.lw, 16)
 
     g.vector.wait_ge(S.lx, 16)
-    g.vector.quantize_mx(T.xq[:, a:a + W], T.xs[:, a:a + W], T.xt[:, :4 * W]).then_inc(S.qx, 1)
+    g.vector.quantize_mx(T.xq[:, a:a + first], T.xs[:, a:a + first], T.xt[:, :4 * first]).then_inc(S.q0, 1)
+    if split:
+        g.vector.wait_ge(S.lx2, 16)
+        g.vector.quantize_mx(T.xq2[:, :], T.xs2[:, :], T.xt[:, 4 * (W - LEAST):4 * W]).then_inc(S.q1, 1)
+        g.vector.quantize_mx(T.xq3[:, :W], T.xs3[:, :W], T.xt[:, :4 * W]).then_inc(S.q2, 1)
     g.vector.wait_ge(S.lw, 16)
     g.vector.quantize_mx(T.wq[:, :], T.ws[:, :], T.wt[:, :]).then_inc(S.qw, 1)
 
-    sent = 0
-    if others:
-        g.wait_ge(S.qx, 1)
+    def mine(p, part):
+        if p == 0:
+            return land(j, pieces(j)[0], part)
+        if part == 0:
+            return T.xq2[:, 2 * LEAST - W:LEAST].bitcast(dt.uint8)
+        return T.xs2[:, 2 * LEAST - W:LEAST]
+
+    def whole(part):
+        if not split:
+            return land(j, (0, W), part)
+        if part == 0:
+            return T.xq3[:, :W].bitcast(dt.uint8)
+        return T.xs3[:, :W]
+
+    whole_sem = S.q2 if split else S.q0
+
+    sentr, sentd = 0, 0
     if relay:
-        for part in (0, 1):
-            trs = []
-            for t, d in enumerate(relay):
-                h = routes[(j, d)][part]
-                rid, pid = topo.addr(h, core)
-                engs = _share(topo, core, h, t)
-                trs.append(RemoteDMATransfer(dst_ids=[DstId(rid=rid, pnc=pid)], dma_engine_mask=_mask(engs),
-                                             remote_sem=S.hin, src=piece(j, part), dst=piece(j, part)))
-                sent += len(engs)
-            g.remote_dma_fused(trs, local_sem=S.sent)
+        for p, run in enumerate(pieces(j)):
+            g.wait_ge(S["q%d" % p], 1)
+            for part in (0, 1):
+                trs = []
+                for t, d in enumerate(relay):
+                    h = routes[(j, d)][part]
+                    rid, pid = topo.addr(h, core)
+                    engs = _share(topo, core, h, t)
+                    trs.append(RemoteDMATransfer(dst_ids=[DstId(rid=rid, pnc=pid)], dma_engine_mask=_mask(engs),
+                                                 remote_sem=S["hin%d" % p], src=mine(p, part), dst=land(j, run, part)))
+                    sentr += len(engs)
+                g.remote_dma_fused(trs, local_sem=S.sentr)
+    if direct:
+        g.wait_ge(whole_sem, 1)
     for part in (0, 1):
         for d in direct:
             rid, pid = topo.addr(cores[d], core)
             m = topo.mask(core, cores[d])
-            g.remote_dma(piece(j, part), piece(j, part), S["arr%d" % slot(j)], S.sent, pid, rid, m)
-            sent += len(_engines(m))
+            g.remote_dma(land(j, (0, W), part), whole(part), S["arr%d_0" % slot(j)], S.sentd, pid, rid, m)
+            sentd += len(_engines(m))
 
     need = {}
     for s in others:
@@ -141,42 +177,69 @@ def rank_program(g, core, T, topo):
         else:
             need[s] = sum(len(_engines(topo.mask(c, core))) for c in h)
 
-    order = ([j] + sorted([s for s in others if routes[(s, j)] is None], key=lambda s: wid[s])
-             + sorted([s for s in others if routes[(s, j)] is not None], key=lambda s: wid[s]))
+    near = [s for s in others if routes[(s, j)] is None]
+    farr = [s for s in others if routes[(s, j)] is not None]
+
+    def runs(s):
+        return pieces(s) if s in farr else [(0, wid[s])]
+
+    def expected(tiles):
+        return sorted([(s, p) for s in tiles for p in range(len(runs(s)))], key=lambda sp: (sp[1], wid[sp[0]]))
+
+    order = [(j, 0)] + expected(near) + expected(farr)
 
     g.tensor.wait_ge(S.qw, 1)
-    g.tensor.wait_ge(S.qx, 1)
-    for s in order:
+    for s, p in order:
         k = slot(s)
-        if s != j:
-            g.tensor.wait_ge(S["arr%d" % k], need[s])
-        g.tensor.matmul_mx(T.ps[:, BANK * k:BANK * k + wid[s]], T.wq[:, :], T.ws[:, :],
-                           T.xq[:, SLOT * k:SLOT * k + wid[s]], T.xs[:, SLOT * k:SLOT * k + wid[s]],
-                           True, True).then_inc(S["mm%d" % k], 1)
+        if s == j:
+            g.tensor.wait_ge(whole_sem, 1)
+        else:
+            g.tensor.wait_ge(S["arr%d_%d" % (k, p)], need[s])
+        b = BANK * (2 * k + p)
+        if s == j and split:
+            q, sc, nn = T.xq3[:, :W], T.xs3[:, :W], W
+        elif p == 0:
+            c1 = runs(s)[0][1]
+            q, sc, nn = T.xq[:, SLOT * k:SLOT * k + c1], T.xs[:, SLOT * k:SLOT * k + c1], c1
+        else:
+            lo, hi = SLOT * k + wid[s] - LEAST, SLOT * k + wid[s]
+            q, sc, nn = T.xq[:, lo:hi], T.xs[:, lo:hi], LEAST
+        g.tensor.matmul_mx(T.ps[:, b:b + nn], T.wq[:, :], T.ws[:, :], q, sc, True, True).then_inc(
+            S["mm%d_%d" % (k, p)], 1)
+
+    lane_of = {(j, 0): 0}
+    for i, sp in enumerate(expected(near)):
+        lane_of[sp] = 1 - i % 2
+    for i, sp in enumerate(expected(farr)):
+        lane_of[sp] = i % 2
 
     stores = [0, 0]
-    for idx, s in enumerate(order):
+    for s, p in order:
         k = slot(s)
         o = sum(wid[r] for r in members(j) if r < s)
-        bank = T.ps[:, BANK * k:BANK * k + wid[s]]
-        block = T.yb[:, o:o + wid[s]]
-        lane = idx % 2
+        c0, c1 = runs(s)[p]
+        b = BANK * (2 * k + p) + (0 if p == 0 else 2 * LEAST - wid[s])
+        bank = T.ps[:, b:b + c1 - c0]
+        block = T.yb[:, o + c0:o + c1]
+        lane = lane_of[(s, p)]
         if lane == 0:
-            g.vector.wait_ge(S["mm%d" % k], 1)
-            g.vector.tensor_copy(block, bank).then_inc(S["cp%d" % k], 1)
+            g.vector.wait_ge(S["mm%d_%d" % (k, p)], 1)
+            g.vector.tensor_copy(block, bank).then_inc(S["cp%d_%d" % (k, p)], 1)
             q, st = g.sync, S.st0
         else:
-            g.scalar.wait_ge(S["mm%d" % k], 1)
-            g.scalar.activation(block, bank, ActivationFunctionType.Copy).then_inc(S["cp%d" % k], 1)
+            g.scalar.wait_ge(S["mm%d_%d" % (k, p)], 1)
+            g.scalar.activation(block, bank, ActivationFunctionType.Copy).then_inc(S["cp%d_%d" % (k, p)], 1)
             q, st = g.scalar, S.st1
-        q.wait_ge(S["cp%d" % k], 1)
-        if stores[lane] == 0 and sent:
-            q.wait_ge(S.sent, sent)
-        q.dma_start(T.y[:, o:o + wid[s]], T.yb[:, o:o + wid[s]]).then_inc(st, 16)
+        q.wait_ge(S["cp%d_%d" % (k, p)], 1)
+        if stores[lane] == 0 and sentr:
+            q.wait_ge(S.sentr, sentr)
+        q.dma_start(T.y[:, o + c0:o + c1], T.yb[:, o + c0:o + c1]).then_inc(st, 16)
         stores[lane] += 1
 
     g.sync.wait_ge(S.st0, 16 * stores[0])
     if stores[1]:
         g.scalar.wait_ge(S.st1, 16 * stores[1])
-    if sent:
-        g.wait_ge(S.sent, sent)
+    if sentr:
+        g.wait_ge(S.sentr, sentr)
+    if sentd:
+        g.wait_ge(S.sentd, sentd)

from concourse.bass import DstId, RemoteDMATransfer
from concourse.mybir import dt, ActivationFunctionType

NSIM = 256
SLOT = 256
NSLOT = 4
BANK = 512
YW = 828
LEAST = 128
MINP2 = 32

SCRATCH = {
    "xt": ("sbuf", [128, 4 * SLOT], "bfloat16"),
    "wt": ("sbuf", [128, 512], "bfloat16"),
    "wq": ("sbuf", [128, 128], "float8_e4m3fn_x4"),
    "ws": ("sbuf", [128, 128], "uint8"),
    "xq": ("sbuf", [128, NSLOT * SLOT], "float8_e4m3fn_x4"),
    "xs": ("sbuf", [128, NSLOT * SLOT], "uint8"),
    "xq2": ("sbuf", [128, LEAST], "float8_e4m3fn_x4"),
    "xs2": ("sbuf", [128, LEAST], "uint8"),
    "xq3": ("sbuf", [128, SLOT], "float8_e4m3fn_x4"),
    "xs3": ("sbuf", [128, SLOT], "uint8"),
    "yb": ("sbuf", [128, YW], "float32"),
    "ps": ("psum", [128, 2 * NSLOT * BANK], "float32"),
}
SEMAPHORES = (["lx", "lx2", "lw", "q0", "q1", "q2", "qw", "hin0", "hin1", "sentr", "sentd", "st0", "st1"]
              + ["%s%d_%d" % (nm, k, p) for nm in ("arr", "mm", "cp") for k in range(NSLOT) for p in range(2)])


def _engines(mask):
    return [e for e in range(mask.bit_length()) if (mask >> e) & 1]


def _mask(engs):
    m = 0
    for e in engs:
        m |= 1 << e
    return m


def _plan(T, topo):
    cores, seq = list(T.cores), T.tables["SEQ"]
    n = len(cores)

    def peers(j):
        return [d for d in range(n) if d != j and seq[d] == seq[j]]

    far = [[d for d in peers(j) if not topo.may_write(cores[j], cores[d])] for j in range(n)]
    routes = {}
    for j in range(n):
        home = cores[j]
        for d in peers(j):
            if d not in far[j]:
                routes[(j, d)] = None
                continue
            i = far[j].index(d)
            p = [s for s in peers(d) if d in far[s]].index(j)
            able = [c for c in range(NSIM) if c not in cores
                    and topo.host(c) == topo.host(home) and topo.chip(c) == topo.chip(home)
                    and topo.may_write(home, c) and topo.may_write(c, cores[d])]
            own = [c for c in able if topo.die(c) == topo.die(home)]
            other = [c for c in able if topo.die(c) != topo.die(home)]
            pick = own if (i + p) % 2 == 0 else other
            routes[(j, d)] = (pick[0], pick[1])
    return routes


def _share(topo, src, dst, t):
    return _engines(topo.mask(src, dst))[t % 2::2]


def rank_program(g, core, T, topo):
    cores, seq, wid = list(T.cores), T.tables["SEQ"], T.tables["WID"]
    n = len(cores)
    S = T.sem
    routes = _plan(T, topo)

    def members(j):
        return [r for r in range(n) if seq[r] == seq[j]]

    def slot(j):
        return members(j).index(j)

    def pieces(j):
        if wid[j] - LEAST < MINP2 or not [d for d in members(j) if d != j and routes[(j, d)] is not None]:
            return [(0, wid[j])]
        return [(0, LEAST), (LEAST, wid[j])]

    def land(j, run, part):
        a = slot(j) * SLOT
        if part == 0:
            return T.xq[:, a + run[0]:a + run[1]].bitcast(dt.uint8)
        return T.xs[:, a + run[0]:a + run[1]]

    rank = T.rank_of(core)

    if rank is None:
        for (j, d), h in routes.items():
            if h is None or core not in h:
                continue
            part = h.index(core)
            t = [x for x in members(j) if x != j and routes[(j, x)] is not None].index(d)
            rid, pid = topo.addr(cores[d], core)
            m = topo.mask(core, cores[d])
            for p, run in enumerate(pieces(j)):
                g.wait_ge(S["hin%d" % p], len(_share(topo, cores[j], core, t)))
                g.remote_dma(land(j, run, part), land(j, run, part), S["arr%d_%d" % (slot(j), p)], S.sentr, pid, rid, m)
            g.wait_ge(S.sentr, len(pieces(j)) * len(_engines(m)))
        return

    j, W = rank, wid[rank]
    a = slot(j) * SLOT
    split = len(pieces(j)) == 2
    others = [d for d in members(j) if d != j]
    relay = [d for d in others if routes[(j, d)] is not None]
    direct = [d for d in others if routes[(j, d)] is None]
    first = pieces(j)[0][1]

    g.sync.dma_start(T.xt[:, :4 * first], T.x[:, :4 * first]).then_inc(S.lx, 16)
    if split:
        g.scalar.dma_start(T.xt[:, 4 * first:4 * W], T.x[:, 4 * first:4 * W]).then_inc(S.lx2, 16)
    g.sync.dma_start(T.wt[:, :], T.w[:, :]).then_inc(S.lw, 16)

    g.vector.wait_ge(S.lx, 16)
    g.vector.quantize_mx(T.xq[:, a:a + first], T.xs[:, a:a + first], T.xt[:, :4 * first]).then_inc(S.q0, 1)
    if split:
        g.vector.wait_ge(S.lx2, 16)
        g.vector.quantize_mx(T.xq2[:, :], T.xs2[:, :], T.xt[:, 4 * (W - LEAST):4 * W]).then_inc(S.q1, 1)
        g.vector.quantize_mx(T.xq3[:, :W], T.xs3[:, :W], T.xt[:, :4 * W]).then_inc(S.q2, 1)
    g.vector.wait_ge(S.lw, 16)
    g.vector.quantize_mx(T.wq[:, :], T.ws[:, :], T.wt[:, :]).then_inc(S.qw, 1)

    def mine(p, part):
        if p == 0:
            return land(j, pieces(j)[0], part)
        if part == 0:
            return T.xq2[:, 2 * LEAST - W:LEAST].bitcast(dt.uint8)
        return T.xs2[:, 2 * LEAST - W:LEAST]

    def whole(part):
        if not split:
            return land(j, (0, W), part)
        if part == 0:
            return T.xq3[:, :W].bitcast(dt.uint8)
        return T.xs3[:, :W]

    whole_sem = S.q2 if split else S.q0

    sentr, sentd = 0, 0
    if relay:
        for p, run in enumerate(pieces(j)):
            g.wait_ge(S["q%d" % p], 1)
            for part in (0, 1):
                trs = []
                for t, d in enumerate(relay):
                    h = routes[(j, d)][part]
                    rid, pid = topo.addr(h, core)
                    engs = _share(topo, core, h, t)
                    trs.append(RemoteDMATransfer(dst_ids=[DstId(rid=rid, pnc=pid)], dma_engine_mask=_mask(engs),
                                                 remote_sem=S["hin%d" % p], src=mine(p, part), dst=land(j, run, part)))
                    sentr += len(engs)
                g.remote_dma_fused(trs, local_sem=S.sentr)
    if direct:
        g.wait_ge(whole_sem, 1)
    for part in (0, 1):
        for d in direct:
            rid, pid = topo.addr(cores[d], core)
            m = topo.mask(core, cores[d])
            g.remote_dma(land(j, (0, W), part), whole(part), S["arr%d_0" % slot(j)], S.sentd, pid, rid, m)
            sentd += len(_engines(m))

    need = {}
    for s in others:
        h = routes[(s, j)]
        if h is None:
            need[s] = 2 * len(_engines(topo.mask(cores[s], core)))
        else:
            need[s] = sum(len(_engines(topo.mask(c, core))) for c in h)

    near = [s for s in others if routes[(s, j)] is None]
    farr = [s for s in others if routes[(s, j)] is not None]

    def runs(s):
        return pieces(s) if s in farr else [(0, wid[s])]

    def expected(tiles):
        return sorted([(s, p) for s in tiles for p in range(len(runs(s)))], key=lambda sp: (sp[1], wid[sp[0]]))

    order = [(j, 0)] + expected(near) + expected(farr)

    g.tensor.wait_ge(S.qw, 1)
    for s, p in order:
        k = slot(s)
        if s == j:
            g.tensor.wait_ge(whole_sem, 1)
        else:
            g.tensor.wait_ge(S["arr%d_%d" % (k, p)], need[s])
        b = BANK * (2 * k + p)
        if s == j and split:
            q, sc, nn = T.xq3[:, :W], T.xs3[:, :W], W
        elif p == 0:
            c1 = runs(s)[0][1]
            q, sc, nn = T.xq[:, SLOT * k:SLOT * k + c1], T.xs[:, SLOT * k:SLOT * k + c1], c1
        else:
            lo, hi = SLOT * k + wid[s] - LEAST, SLOT * k + wid[s]
            q, sc, nn = T.xq[:, lo:hi], T.xs[:, lo:hi], LEAST
        g.tensor.matmul_mx(T.ps[:, b:b + nn], T.wq[:, :], T.ws[:, :], q, sc, True, True).then_inc(
            S["mm%d_%d" % (k, p)], 1)

    lane_of = {(j, 0): 0}
    for i, sp in enumerate(expected(near)):
        lane_of[sp] = 1 - i % 2
    for i, sp in enumerate(expected(farr)):
        lane_of[sp] = i % 2

    stores = [0, 0]
    for s, p in order:
        k = slot(s)
        o = sum(wid[r] for r in members(j) if r < s)
        c0, c1 = runs(s)[p]
        b = BANK * (2 * k + p) + (0 if p == 0 else 2 * LEAST - wid[s])
        bank = T.ps[:, b:b + c1 - c0]
        block = T.yb[:, o + c0:o + c1]
        lane = lane_of[(s, p)]
        if lane == 0:
            g.vector.wait_ge(S["mm%d_%d" % (k, p)], 1)
            g.vector.tensor_copy(block, bank).then_inc(S["cp%d_%d" % (k, p)], 1)
            q, st = g.sync, S.st0
        else:
            g.scalar.wait_ge(S["mm%d_%d" % (k, p)], 1)
            g.scalar.activation(block, bank, ActivationFunctionType.Copy).then_inc(S["cp%d_%d" % (k, p)], 1)
            q, st = g.scalar, S.st1
        q.wait_ge(S["cp%d_%d" % (k, p)], 1)
        if stores[lane] == 0 and sentr:
            q.wait_ge(S.sentr, sentr)
        q.dma_start(T.y[:, o + c0:o + c1], T.yb[:, o + c0:o + c1]).then_inc(st, 16)
        stores[lane] += 1

    g.sync.wait_ge(S.st0, 16 * stores[0])
    if stores[1]:
        g.scalar.wait_ge(S.st1, 16 * stores[1])
    if sentr:
        g.wait_ge(S.sentr, sentr)
    if sentd:
        g.wait_ge(S.sentd, sentd)
